import numpy as np
import ml_dtypes


def mxq(x, axis, fmt="e4m3"):
    dtype, down = {"e4m3": (ml_dtypes.float8_e4m3fn, 7), "e5m2": (ml_dtypes.float8_e5m2, 14)}[fmt]
    v = np.moveaxis(np.asarray(x, np.float32).astype(ml_dtypes.bfloat16).astype(np.float64), axis, -1)
    blocks = v.reshape(v.shape[:-1] + (-1, 32))
    amax = np.abs(blocks).max(-1, keepdims=True)
    byte = np.maximum(np.where(amax > 0, np.frexp(amax)[1] - 1 + 127, 0) - down, 1)
    scale = np.exp2(byte - 127.0)
    codes = (blocks / scale).astype(np.float32).astype(dtype).astype(np.float64)
    return np.moveaxis((codes * scale).reshape(v.shape), -1, axis)


WIDE = False


def mx_kscale(k):
    if not WIDE:
        return np.ones(k)
    levels = np.array([10, -10, 5, -5, 0])
    if k % 512:
        return np.exp2(np.random.permutation(np.resize(levels, k // 32))).repeat(32)
    a = np.empty((k // 512, 16))
    for p in range(k // 512):
        a[p, :8] = np.random.permutation(np.resize(levels, 8))
        for g in range(8):
            far = levels[np.abs(levels - a[p, g]) >= 10]
            a[p, g + 8] = far[np.random.randint(len(far))]
    return np.exp2(a.ravel()).repeat(32)


def f64(x):
    return np.asarray(x).astype(np.float64)


def striped(idx):
    return np.tile(idx.reshape(-1, 16).T, (8, 1)).astype(np.uint16)


def unstriped(offs):
    return offs[:16].T.reshape(-1).astype(np.int64)


def pack_weight(w):
    k, n = w.shape
    w = f64(np.asarray(w, np.float32).astype(ml_dtypes.bfloat16)).reshape(k // 32, 32, n)
    amax = np.abs(w).max(1)
    byte = np.clip(np.where(amax > 0, np.frexp(amax)[1] - 1 + 127 - 7, 1), 1, 254)
    scaled = (w * np.exp2(127.0 - byte)[:, None, :]).reshape(k, n).astype(np.float32)
    words = np.ascontiguousarray(scaled.reshape(k // 512, 128, 4, n).transpose(0, 1, 3, 2)).astype(ml_dtypes.float8_e4m3fn).view(np.uint8)
    return words, np.ascontiguousarray(byte.astype(np.uint8).reshape(k // 512, 16, n))


def unpack_weight(words, scales):
    g, p, n, _ = words.shape
    vals = np.ascontiguousarray(words).view(ml_dtypes.float8_e4m3fn).astype(np.float64) * np.repeat(np.exp2(scales.astype(np.float64) - 127.0), 8, axis=1)[..., None]
    return vals.transpose(0, 1, 3, 2).reshape(g * 512, n)


def relu(v):
    return np.maximum(v, 0.0)


K, T, S, H, N = 512, 1024, 512, 512, 256


def setup_inputs():
    n = np.random.standard_normal
    s = mx_kscale(K)[:, None]
    u = mx_kscale(H)
    packed_xT = pack_weight(n((K, T)) * s)
    return {
        "x_words": packed_xT[0],
        "x_scales": packed_xT[1],
        "w1": (n((K, H)) / np.sqrt(K) / s * u).astype(np.float32),
        "w2": (n((H, N)) / np.sqrt(H) / u[:, None]).astype(np.float32),
        "offs": striped(np.random.permutation(T)[:S]),
    }


def reference(x_words, x_scales, w1, w2, offs):
    xq = unpack_weight(x_words, x_scales)[:, unstriped(offs)]
    h = relu(mxq(f64(w1), 0, "e4m3").T @ xq)
    z = h - h.mean(axis=1, keepdims=True)
    return mxq(f64(w2), 0, "e4m3").T @ mxq(z, 0, "e4m3")

@@ -1,0 +1,117 @@
+from contextlib import ExitStack
+
+import concourse.mybir as mybir
+
+K, T, S, H, N = 512, 1024, 512, 512, 256
+FLOPS = 2 * K * H * S + 2 * H * N * S
+
+F32 = mybir.dt.float32
+BF16 = mybir.dt.bfloat16
+I32 = mybir.dt.int32
+U32 = mybir.dt.uint32
+U16 = mybir.dt.uint16
+U8 = mybir.dt.uint8
+FP8X4 = mybir.dt.float8_e4m3fn_x4
+ALU = mybir.AluOpType
+ACT = mybir.ActivationFunctionType
+
+P = 128
+PACK = 4
+HALF = H // 2
+CH = 256
+VCOLS = 160
+
+
+def tile_picked_deepset_relu_p_kernel(tc, x_words, x_scales, w1, w2, offs, out):
+    nc = tc.nc
+    with ExitStack() as ctx:
+        sb = ctx.enter_context(tc.tile_pool(name="sb", bufs=1))
+        ps = ctx.enter_context(tc.psum_pool(name="ps", bufs=1))
+
+        offsets = sb.tile([P, S // 16], U16, name="offsets")
+        nc.sync.dma_start(offsets[:], offs)
+
+        xw = sb.tile([P, T], I32, name="xw", align_bytes=64)
+        nc.sync.dma_start(xw[:], x_words[0].rearrange("p c r -> p (c r)").bitcast(I32))
+
+        xs = sb.tile([P, T], U8, name="xs", align_bytes=64)
+        nc.vector.memset(xs[:].bitcast(I32), 0)
+        for q in range(4):
+            nc.scalar.dma_start(xs[32 * q : 32 * q + 4, :].bitcast(I32), x_scales[0, 4 * q : 4 * q + 4, :].bitcast(I32))
+
+        w1_rows = w1.rearrange("(p j) c -> p j c", j=PACK)
+        w1_raw = []
+        for a in range(2):
+            raw = sb.tile([P, PACK, HALF], F32, name="w1_raw%d" % a, align_bytes=64)
+            nc.sync.dma_start(raw[:], w1_rows[:, :, a * HALF : (a + 1) * HALF])
+            w1_raw.append(raw)
+        w2_raw = sb.tile([P, PACK, N], F32, name="w2_raw", align_bytes=64)
+        nc.sync.dma_start(w2_raw[:], w2.rearrange("(p j) c -> p j c", j=PACK))
+
+        xg = sb.tile([P, S], U32, name="xg", align_bytes=64)
+        nc.vector.tensor_copy(xg[:], xw[:].bitcast(U32).indirect(offsets[:]))
+        xsg = sb.tile([P, S], U8, name="xsg", align_bytes=64)
+        nc.vector.tensor_copy(xsg[:], xs[:].indirect(offsets[:]))
+
+        w1_bf = sb.tile([P, PACK, P, PACK], BF16, name="w1_bf", align_bytes=64)
+
+        def cast_w1(copy, a, c0, c1):
+            m0, m1 = (a * HALF + c0) // PACK, (a * HALF + c1) // PACK
+            copy(
+                w1_bf[:, :, m0:m1, :].rearrange("p t m j -> p m j t"),
+                w1_raw[a][:, :, c0:c1].rearrange("p j (m t) -> p m j t", t=PACK),
+            )
+
+        cast_w1(nc.scalar.copy, 0, 0, HALF)
+        cast_w1(nc.vector.tensor_copy, 1, 0, VCOLS)
+        cast_w1(nc.scalar.copy, 1, VCOLS, HALF)
+
+        w1_codes, w1_scales = [], []
+        for t in range(PACK):
+            codes = sb.tile([P, P], U32, name="w1_codes%d" % t, align_bytes=64)
+            scales = sb.tile([P, P], U8, name="w1_scales%d" % t, align_bytes=64)
+            nc.vector.quantize_mx(codes[:].bitcast(FP8X4), scales[:], w1_bf[:, t].rearrange("p m j -> p (m j)"))
+            w1_codes.append(codes)
+            w1_scales.append(scales)
+
+        w2_bf = sb.tile([P, N, PACK], BF16, name="w2_bf", align_bytes=64)
+        nc.vector.tensor_copy(
+            w2_bf[:].rearrange("p (c i) j -> p c j i", i=4),
+            w2_raw[:].rearrange("p j (c i) -> p c j i", i=4),
+        )
+        w2_codes = sb.tile([P, N], U32, name="w2_codes", align_bytes=64)
+        w2_scales = sb.tile([P, N], U8, name="w2_scales", align_bytes=64)
+        nc.vector.quantize_mx(w2_codes[:].bitcast(FP8X4), w2_scales[:], w2_bf[:].rearrange("p c j -> p (c j)"))
+
+        nch = S // CH
+        pairs = [sb.tile([P, 2, CH, 2], BF16, name="pairs%d" % c, align_bytes=64) for c in range(nch)]
+        for t in range(PACK):
+            acc = ps.tile([P, S], F32, name="acc%d" % t)
+            nc.tensor.matmul_mx(acc[:], lhsT=w1_codes[t][:].bitcast(FP8X4), lhsT_scale=w1_scales[t][:],
+                                rhs=xg[:].bitcast(FP8X4), rhs_scale=xsg[:], start=True, stop=True)
+            h = sb.tile([P, S], F32, name="h%d" % t, align_bytes=64)
+            total = sb.tile([P, 1], F32, name="total%d" % t)
+            nc.scalar.activation(h[:], acc[:], ACT.Relu, accum_out=total[:])
+            for c in range(nch):
+                nc.vector.tensor_scalar(pairs[c][:, t // 2, :, t % 2], h[:, c * CH : (c + 1) * CH], -float(S), total[:],
+                                        ALU.mult, ALU.add)
+
+        for c in range(nch):
+            z = sb.tile([P, CH * PACK], BF16, name="z%d" % c, align_bytes=64)
+            copy = nc.vector.tensor_copy if c == 0 else nc.scalar.copy
+            copy(z[:].bitcast(F32).rearrange("p (n u) -> p n u", u=2),
+                 pairs[c][:].rearrange("p u n e -> p u (n e)").bitcast(F32).rearrange("p u n -> p n u"))
+            z_codes = sb.tile([P, CH], U32, name="z_codes%d" % c, align_bytes=64)
+            z_scales = sb.tile([P, CH], U8, name="z_scales%d" % c, align_bytes=64)
+            nc.vector.quantize_mx(z_codes[:].bitcast(FP8X4), z_scales[:], z[:])
+            for m in range(N // P):
+                acc2 = ps.tile([P, CH], F32, name="acc2_%d_%d" % (c, m))
+                nc.tensor.matmul_mx(acc2[:], lhsT=w2_codes[:, m * P : (m + 1) * P].bitcast(FP8X4),
+                                    lhsT_scale=w2_scales[:, m * P : (m + 1) * P],
+                                    rhs=z_codes[:].bitcast(FP8X4), rhs_scale=z_scales[:], start=True, stop=True)
+                res = sb.tile([P, CH], F32, name="res%d_%d" % (c, m))
+                if m == 0:
+                    nc.scalar.activation(res[:], acc2[:], ACT.Copy, scale=-1.0 / S)
+                else:
+                    nc.vector.tensor_scalar(res[:], acc2[:], -1.0 / S, None, ALU.mult)
+                nc.sync.dma_start(out[m * P : (m + 1) * P, c * CH : (c + 1) * CH], res[:])

@@ -18,7 +18,7 @@ ACT = mybir.ActivationFunctionType
 P = 128
 PACK = 4
 HALF = H // 2
-CH = 256
+CH = 128
 VCOLS = 160
 
 
@@ -28,16 +28,15 @@ def tile_picked_deepset_relu_p_kernel(tc, x_words, x_scales, w1, w2, offs, out):
         sb = ctx.enter_context(tc.tile_pool(name="sb", bufs=1))
         ps = ctx.enter_context(tc.psum_pool(name="ps", bufs=1))
 
-        offsets = sb.tile([P, S // 16], U16, name="offsets")
-        nc.sync.dma_start(offsets[:], offs)
-
         xw = sb.tile([P, T], I32, name="xw", align_bytes=64)
         nc.sync.dma_start(xw[:], x_words[0].rearrange("p c r -> p (c r)").bitcast(I32))
+        offsets = sb.tile([P, S // 16], U16, name="offsets")
+        nc.sync.dma_start(offsets[:], offs)
 
         xs = sb.tile([P, T], U8, name="xs", align_bytes=64)
         nc.vector.memset(xs[:].bitcast(I32), 0)
         for q in range(4):
-            nc.scalar.dma_start(xs[32 * q : 32 * q + 4, :].bitcast(I32), x_scales[0, 4 * q : 4 * q + 4, :].bitcast(I32))
+            nc.sync.dma_start(xs[32 * q : 32 * q + 4, :].bitcast(I32), x_scales[0, 4 * q : 4 * q + 4, :].bitcast(I32))
 
         w1_rows = w1.rearrange("(p j) c -> p j c", j=PACK)
         w1_raw = []
@@ -74,19 +73,19 @@ def tile_picked_deepset_relu_p_kernel(tc, x_words, x_scales, w1, w2, offs, out):
             w1_codes.append(codes)
             w1_scales.append(scales)
 
-        w2_bf = sb.tile([P, N, PACK], BF16, name="w2_bf", align_bytes=64)
+        w2_bf = w1_bf[:, 2:4].rearrange("p t m j -> p (t m) j")
         nc.vector.tensor_copy(
-            w2_bf[:].rearrange("p (c i) j -> p c j i", i=4),
+            w2_bf.rearrange("p (c i) j -> p c j i", i=4),
             w2_raw[:].rearrange("p j (c i) -> p c j i", i=4),
         )
         w2_codes = sb.tile([P, N], U32, name="w2_codes", align_bytes=64)
         w2_scales = sb.tile([P, N], U8, name="w2_scales", align_bytes=64)
-        nc.vector.quantize_mx(w2_codes[:].bitcast(FP8X4), w2_scales[:], w2_bf[:].rearrange("p c j -> p (c j)"))
+        nc.vector.quantize_mx(w2_codes[:].bitcast(FP8X4), w2_scales[:], w2_bf.rearrange("p c j -> p (c j)"))
 
         nch = S // CH
         pairs = [sb.tile([P, 2, CH, 2], BF16, name="pairs%d" % c, align_bytes=64) for c in range(nch)]
         for t in range(PACK):
-            acc = ps.tile([P, S], F32, name="acc%d" % t)
+            acc = ps.tile([P, S], F32, name="acc%d" % t, tag="bank%d" % t)
             nc.tensor.matmul_mx(acc[:], lhsT=w1_codes[t][:].bitcast(FP8X4), lhsT_scale=w1_scales[t][:],
                                 rhs=xg[:].bitcast(FP8X4), rhs_scale=xsg[:], start=True, stop=True)
             h = sb.tile([P, S], F32, name="h%d" % t, align_bytes=64)
@@ -96,22 +95,39 @@ def tile_picked_deepset_relu_p_kernel(tc, x_words, x_scales, w1, w2, offs, out):
                 nc.vector.tensor_scalar(pairs[c][:, t // 2, :, t % 2], h[:, c * CH : (c + 1) * CH], -float(S), total[:],
                                         ALU.mult, ALU.add)
 
+        out_rows = out.rearrange("(m p) n -> p m n", p=P)
+        zs = []
         for c in range(nch):
             z = sb.tile([P, CH * PACK], BF16, name="z%d" % c, align_bytes=64)
-            copy = nc.vector.tensor_copy if c == 0 else nc.scalar.copy
+            copy = nc.vector.tensor_copy if c < 2 else nc.scalar.copy
             copy(z[:].bitcast(F32).rearrange("p (n u) -> p n u", u=2),
                  pairs[c][:].rearrange("p u n e -> p u (n e)").bitcast(F32).rearrange("p u n -> p n u"))
+            zs.append(z)
+
+        def leave(engine, dst, src):
+            if engine == "scalar":
+                nc.scalar.activation(dst, src, ACT.Copy, scale=-1.0 / S)
+            else:
+                nc.vector.tensor_scalar(dst, src, -1.0 / S, None, ALU.mult)
+
+        for c in range(nch):
             z_codes = sb.tile([P, CH], U32, name="z_codes%d" % c, align_bytes=64)
             z_scales = sb.tile([P, CH], U8, name="z_scales%d" % c, align_bytes=64)
-            nc.vector.quantize_mx(z_codes[:].bitcast(FP8X4), z_scales[:], z[:])
-            for m in range(N // P):
-                acc2 = ps.tile([P, CH], F32, name="acc2_%d_%d" % (c, m))
-                nc.tensor.matmul_mx(acc2[:], lhsT=w2_codes[:, m * P : (m + 1) * P].bitcast(FP8X4),
+            nc.vector.quantize_mx(z_codes[:].bitcast(FP8X4), z_scales[:], zs[c][:])
+            res = sb.tile([P, 2, CH], F32, name="res%d" % c)
+            last = c == nch - 1
+            if last:
+                banks = [ps.tile([P, CH], F32, name="acc2_%d_%d" % (c, m), tag="bank%d" % (7 * m))[:] for m in range(2)]
+            else:
+                both = ps.tile([P, 2, CH], F32, name="acc2_%d" % c, tag="bank%d" % (4 + c))
+                banks = [both[:, m, :] for m in range(2)]
+            for m in range(2):
+                nc.tensor.matmul_mx(banks[m], lhsT=w2_codes[:, m * P : (m + 1) * P].bitcast(FP8X4),
                                     lhsT_scale=w2_scales[:, m * P : (m + 1) * P],
                                     rhs=z_codes[:].bitcast(FP8X4), rhs_scale=z_scales[:], start=True, stop=True)
-                res = sb.tile([P, CH], F32, name="res%d_%d" % (c, m))
-                if m == 0:
-                    nc.scalar.activation(res[:], acc2[:], ACT.Copy, scale=-1.0 / S)
-                else:
-                    nc.vector.tensor_scalar(res[:], acc2[:], -1.0 / S, None, ALU.mult)
-                nc.sync.dma_start(out[m * P : (m + 1) * P, c * CH : (c + 1) * CH], res[:])
+            if last:
+                leave("scalar", res[:, 0, :], banks[0])
+                leave("vector", res[:, 1, :], banks[1])
+            else:
+                leave("scalar" if c < 2 else "vector", res[:], both[:])
+            nc.sync.dma_start(out_rows[:, :, c * CH : (c + 1) * CH], res[:])

@@ -95,6 +95,10 @@ def tile_picked_deepset_relu_p_kernel(tc, x_words, x_scales, w1, w2, offs, out):
                 nc.vector.tensor_scalar(pairs[c][:, t // 2, :, t % 2], h[:, c * CH : (c + 1) * CH], -float(S), total[:],
                                         ALU.mult, ALU.add)
 
+        for bank, width in ((5, S), (6, S // 2)):
+            spare = ps.tile([P, width], F32, name="spare%d" % bank, tag="bank%d" % bank)
+            nc.tensor.matmul_mx(spare[:], lhsT=w1_codes[3][:].bitcast(FP8X4), lhsT_scale=w1_scales[3][:],
+                                rhs=xg[:, :width].bitcast(FP8X4), rhs_scale=xsg[:, :width], start=True, stop=True)
         out_rows = out.rearrange("(m p) n -> p m n", p=P)
         zs = []
         for c in range(nch):

@@ -19,7 +19,7 @@ P = 128
 PACK = 4
 HALF = H // 2
 CH = 128
-VCOLS = 160
+SH = S // 2
 
 
 def tile_picked_deepset_relu_p_kernel(tc, x_words, x_scales, w1, w2, offs, out):
@@ -28,84 +28,109 @@ def tile_picked_deepset_relu_p_kernel(tc, x_words, x_scales, w1, w2, offs, out):
         sb = ctx.enter_context(tc.tile_pool(name="sb", bufs=1))
         ps = ctx.enter_context(tc.psum_pool(name="ps", bufs=1))
 
-        xw = sb.tile([P, T], I32, name="xw", align_bytes=64)
-        nc.sync.dma_start(xw[:], x_words[0].rearrange("p c r -> p (c r)").bitcast(I32))
+        w1_rows = w1.rearrange("(p j) c -> p j c", j=PACK)
+        w1_raw = [sb.tile([P, PACK, HALF], F32, name="w1_raw%d" % a, align_bytes=64) for a in range(2)]
+        nc.sync.dma_start(w1_raw[0][:], w1_rows[:, :, :HALF])
         offsets = sb.tile([P, S // 16], U16, name="offsets")
         nc.sync.dma_start(offsets[:], offs)
-
         xs = sb.tile([P, T], U8, name="xs", align_bytes=64)
         nc.vector.memset(xs[:].bitcast(I32), 0)
         for q in range(4):
             nc.sync.dma_start(xs[32 * q : 32 * q + 4, :].bitcast(I32), x_scales[0, 4 * q : 4 * q + 4, :].bitcast(I32))
+        nc.sync.dma_start(w1_raw[1][:], w1_rows[:, :, HALF:])
+        xw = sb.tile([P, T], I32, name="xw", align_bytes=64)
+        nc.sync.dma_start(xw[:], x_words[0].rearrange("p c r -> p (c r)").bitcast(I32))
+        w2_rows = w2.rearrange("(p j) c -> p j c", j=PACK)
+        w2_raw = [sb.tile([P, PACK, P], F32, name="w2_raw%d" % m, align_bytes=64) for m in range(2)]
+        for m in range(2):
+            nc.sync.dma_start(w2_raw[m][:], w2_rows[:, :, m * P : (m + 1) * P])
 
-        w1_rows = w1.rearrange("(p j) c -> p j c", j=PACK)
-        w1_raw = []
-        for a in range(2):
-            raw = sb.tile([P, PACK, HALF], F32, name="w1_raw%d" % a, align_bytes=64)
-            nc.sync.dma_start(raw[:], w1_rows[:, :, a * HALF : (a + 1) * HALF])
-            w1_raw.append(raw)
-        w2_raw = sb.tile([P, PACK, N], F32, name="w2_raw", align_bytes=64)
-        nc.sync.dma_start(w2_raw[:], w2.rearrange("(p j) c -> p j c", j=PACK))
-
-        xg = sb.tile([P, S], U32, name="xg", align_bytes=64)
-        nc.vector.tensor_copy(xg[:], xw[:].bitcast(U32).indirect(offsets[:]))
         xsg = sb.tile([P, S], U8, name="xsg", align_bytes=64)
         nc.vector.tensor_copy(xsg[:], xs[:].indirect(offsets[:]))
+        xg = sb.tile([P, S], U32, name="xg", align_bytes=64)
+        for g in range(2):
+            nc.vector.tensor_copy(xg[:, g * SH : (g + 1) * SH],
+                                  xw[:].bitcast(U32).indirect(offsets[:, g * SH // 16 : (g + 1) * SH // 16]))
 
-        w1_bf = sb.tile([P, PACK, P, PACK], BF16, name="w1_bf", align_bytes=64)
+        MH = HALF // PACK
 
-        def cast_w1(copy, a, c0, c1):
-            m0, m1 = (a * HALF + c0) // PACK, (a * HALF + c1) // PACK
+        def cast_w1(copy, a, t0, t1):
+            whole = sb.tile([P, PACK, MH, PACK], BF16, name="w1_bf%d_%d" % (a, t0), align_bytes=64)
+            bf = whole[:, : t1 - t0]
             copy(
-                w1_bf[:, :, m0:m1, :].rearrange("p t m j -> p m j t"),
-                w1_raw[a][:, :, c0:c1].rearrange("p j (m t) -> p m j t", t=PACK),
+                bf.rearrange("p t m j -> p m j t"),
+                w1_raw[a][:].rearrange("p j (m t) -> p m j t", t=PACK)[:, :, :, t0:t1],
             )
+            return whole
 
-        cast_w1(nc.scalar.copy, 0, 0, HALF)
-        cast_w1(nc.vector.tensor_copy, 1, 0, VCOLS)
-        cast_w1(nc.scalar.copy, 1, VCOLS, HALF)
+        first_low = cast_w1(nc.vector.tensor_copy, 0, 0, 2)
+        first_high = cast_w1(nc.scalar.copy, 0, 2, PACK)
+        low = cast_w1(nc.scalar.copy, 1, 0, 2)
+        high = cast_w1(nc.scalar.copy, 1, 2, PACK)
 
         w1_codes, w1_scales = [], []
         for t in range(PACK):
             codes = sb.tile([P, P], U32, name="w1_codes%d" % t, align_bytes=64)
             scales = sb.tile([P, P], U8, name="w1_scales%d" % t, align_bytes=64)
-            nc.vector.quantize_mx(codes[:].bitcast(FP8X4), scales[:], w1_bf[:, t].rearrange("p m j -> p (m j)"))
+            second = low[:, t] if t < 2 else high[:, t - 2]
+            first = first_low[:, t] if t < 2 else first_high[:, t - 2]
+            for a, part in enumerate((first, second)):
+                nc.vector.quantize_mx(codes[:, a * MH : (a + 1) * MH].bitcast(FP8X4), scales[:, a * MH : (a + 1) * MH],
+                                      part.rearrange("p m j -> p (m j)"))
             w1_codes.append(codes)
             w1_scales.append(scales)
 
-        w2_bf = w1_bf[:, 2:4].rearrange("p t m j -> p (t m) j")
-        nc.vector.tensor_copy(
-            w2_bf.rearrange("p (c i) j -> p c j i", i=4),
-            w2_raw[:].rearrange("p j (c i) -> p c j i", i=4),
-        )
         w2_codes = sb.tile([P, N], U32, name="w2_codes", align_bytes=64)
         w2_scales = sb.tile([P, N], U8, name="w2_scales", align_bytes=64)
-        nc.vector.quantize_mx(w2_codes[:].bitcast(FP8X4), w2_scales[:], w2_bf.rearrange("p c j -> p (c j)"))
+        w2_first = sb.tile([P, P, PACK], BF16, name="w2_first", align_bytes=64)
+        w2_second = high[:, 0:2].rearrange("p t m j -> p (t m) j")
+        for m, (copy, w2_bf) in enumerate(((nc.scalar.copy, w2_first[:]), (nc.vector.tensor_copy, w2_second))):
+            copy(
+                w2_bf.rearrange("p (c i) j -> p c j i", i=4),
+                w2_raw[m][:].rearrange("p j (c i) -> p c j i", i=4),
+            )
+        for m, w2_bf in ((0, w2_first[:]), (1, w2_second)):
+            nc.vector.quantize_mx(w2_codes[:, m * P : (m + 1) * P].bitcast(FP8X4), w2_scales[:, m * P : (m + 1) * P],
+                                  w2_bf.rearrange("p c j -> p (c j)"))
 
         nch = S // CH
-        pairs = [sb.tile([P, 2, CH, 2], BF16, name="pairs%d" % c, align_bytes=64) for c in range(nch)]
-        for t in range(PACK):
-            acc = ps.tile([P, S], F32, name="acc%d" % t, tag="bank%d" % t)
-            nc.tensor.matmul_mx(acc[:], lhsT=w1_codes[t][:].bitcast(FP8X4), lhsT_scale=w1_scales[t][:],
-                                rhs=xg[:].bitcast(FP8X4), rhs_scale=xsg[:], start=True, stop=True)
-            h = sb.tile([P, S], F32, name="h%d" % t, align_bytes=64)
-            total = sb.tile([P, 1], F32, name="total%d" % t)
-            nc.scalar.activation(h[:], acc[:], ACT.Relu, accum_out=total[:])
-            for c in range(nch):
-                nc.vector.tensor_scalar(pairs[c][:, t // 2, :, t % 2], h[:, c * CH : (c + 1) * CH], -float(S), total[:],
-                                        ALU.mult, ALU.add)
+        pairs = [sb.tile([P, PACK * 2 * CH], BF16, name="pairs%d" % g, align_bytes=64) for g in range(2)]
+        hs = [sb.tile([P, S], F32, name="h%d" % t, align_bytes=64) for t in range(PACK)]
 
-        for bank, width in ((5, S), (6, S // 2)):
-            spare = ps.tile([P, width], F32, name="spare%d" % bank, tag="bank%d" % bank)
-            nc.tensor.matmul_mx(spare[:], lhsT=w1_codes[3][:].bitcast(FP8X4), lhsT_scale=w1_scales[3][:],
-                                rhs=xg[:, :width].bitcast(FP8X4), rhs_scale=xsg[:, :width], start=True, stop=True)
+        def product(t, n0, n1, bank, so_far=None):
+            acc = ps.tile([P, n1 - n0], F32, name="acc%d" % bank, tag="bank%d" % bank)
+            nc.tensor.matmul_mx(acc[:], lhsT=w1_codes[t][:].bitcast(FP8X4), lhsT_scale=w1_scales[t][:],
+                                rhs=xg[:, n0:n1].bitcast(FP8X4), rhs_scale=xsg[:, n0:n1], start=True, stop=True)
+            total = sb.tile([P, 1], F32, name="total%d" % bank)
+            if so_far is None:
+                nc.scalar.activation(hs[t][:, n0:n1], acc[:], ACT.Relu, accum_out=total[:])
+            else:
+                nc.vector.tensor_scalar(hs[t][:, n0:n1], acc[:], 0.0, so_far[:], ALU.max, ALU.add, accum_out=total[:])
+            return total
+
+        def centre(t, total):
+            for g in range(2):
+                nc.vector.tensor_scalar(pairs[g][:].rearrange("p (u n e) -> p u n e", u=2, e=2)[:, t // 2, :, t % 2],
+                                        hs[t][:, g * 2 * CH : (g + 1) * 2 * CH], -float(S), total[:], ALU.mult, ALU.add)
+
+        parts = [product(t, 0, SH, 4 + t) for t in range(2)]
+        both_halves = [product(0, SH, S, 0, parts[0])]
+        rest = product(1, SH, S, 1)
+        total = sb.tile([P, 1], F32, name="sum1")
+        nc.vector.tensor_tensor(total[:], parts[1][:], rest[:], ALU.add)
+        both_halves.append(total)
+        for t in range(PACK):
+            centre(t, both_halves[t] if t < 2 else product(t, 0, S, t))
+        spare = ps.tile([P, S], F32, name="spare", tag="bank6")
+        nc.tensor.matmul_mx(spare[:], lhsT=w1_codes[3][:].bitcast(FP8X4), lhsT_scale=w1_scales[3][:],
+                            rhs=xg[:].bitcast(FP8X4), rhs_scale=xsg[:], start=True, stop=True)
         out_rows = out.rearrange("(m p) n -> p m n", p=P)
         zs = []
         for c in range(nch):
             z = sb.tile([P, CH * PACK], BF16, name="z%d" % c, align_bytes=64)
-            copy = nc.vector.tensor_copy if c < 2 else nc.scalar.copy
+            copy = nc.vector.tensor_copy if c % 2 == 0 else nc.scalar.copy
             copy(z[:].bitcast(F32).rearrange("p (n u) -> p n u", u=2),
-                 pairs[c][:].rearrange("p u n e -> p u (n e)").bitcast(F32).rearrange("p u n -> p n u"))
+                 pairs[c // 2][:].bitcast(F32).rearrange("p (u n) -> p n u", u=2)[:, c % 2 * CH : (c % 2 + 1) * CH, :])
             zs.append(z)
 
         def leave(engine, dst, src):
@@ -118,18 +143,23 @@ def tile_picked_deepset_relu_p_kernel(tc, x_words, x_scales, w1, w2, offs, out):
             z_codes = sb.tile([P, CH], U32, name="z_codes%d" % c, align_bytes=64)
             z_scales = sb.tile([P, CH], U8, name="z_scales%d" % c, align_bytes=64)
             nc.vector.quantize_mx(z_codes[:].bitcast(FP8X4), z_scales[:], zs[c][:])
-            res = sb.tile([P, 2, CH], F32, name="res%d" % c)
-            last = c == nch - 1
-            if last:
-                banks = [ps.tile([P, CH], F32, name="acc2_%d_%d" % (c, m), tag="bank%d" % (7 * m))[:] for m in range(2)]
+            if c in (0, nch - 1):
+                banks = [ps.tile([P, CH], F32, name="acc2_%d_%d" % (c, m), tag="bank%d" % (7 * m if c else 4 + m))[:] for m in range(2)]
             else:
-                both = ps.tile([P, 2, CH], F32, name="acc2_%d" % c, tag="bank%d" % (4 + c))
+                both = ps.tile([P, 2, CH], F32, name="acc2_%d" % c, tag="bank%d" % c)
                 banks = [both[:, m, :] for m in range(2)]
             for m in range(2):
                 nc.tensor.matmul_mx(banks[m], lhsT=w2_codes[:, m * P : (m + 1) * P].bitcast(FP8X4),
                                     lhsT_scale=w2_scales[:, m * P : (m + 1) * P],
                                     rhs=z_codes[:].bitcast(FP8X4), rhs_scale=z_scales[:], start=True, stop=True)
-            if last:
+            if c == 0:
+                for m in range(2):
+                    half = sb.tile([P, CH], F32, name="res0_%d" % m)
+                    leave("scalar", half[:], banks[m])
+                    nc.sync.dma_start(out_rows[:, m, :CH], half[:])
+                continue
+            res = sb.tile([P, 2, CH], F32, name="res%d" % c)
+            if c == nch - 1:
                 leave("scalar", res[:, 0, :], banks[0])
                 leave("vector", res[:, 1, :], banks[1])
             else:

@@ -48,42 +48,38 @@ def tile_picked_deepset_relu_p_kernel(tc, x_words, x_scales, w1, w2, offs, out):
         xsg = sb.tile([P, S], U8, name="xsg", align_bytes=64)
         nc.vector.tensor_copy(xsg[:], xs[:].indirect(offsets[:]))
         xg = sb.tile([P, S], U32, name="xg", align_bytes=64)
-        for g in range(2):
-            nc.vector.tensor_copy(xg[:, g * SH : (g + 1) * SH],
-                                  xw[:].bitcast(U32).indirect(offsets[:, g * SH // 16 : (g + 1) * SH // 16]))
+        for n0 in range(0, S, CH):
+            nc.vector.tensor_copy(xg[:, n0 : n0 + CH], xw[:].bitcast(U32).indirect(offsets[:, n0 // 16 : (n0 + CH) // 16]))
 
         MH = HALF // PACK
 
-        def cast_w1(copy, a, t0, t1):
-            whole = sb.tile([P, PACK, MH, PACK], BF16, name="w1_bf%d_%d" % (a, t0), align_bytes=64)
-            bf = whole[:, : t1 - t0]
-            copy(
-                bf.rearrange("p t m j -> p m j t"),
-                w1_raw[a][:].rearrange("p j (m t) -> p m j t", t=PACK)[:, :, :, t0:t1],
-            )
-            return whole
+        w1_bf = [sb.tile([P, 2, P, PACK], BF16, name="w1_bf%d" % u, align_bytes=64) for u in range(2)]
 
-        first_low = cast_w1(nc.vector.tensor_copy, 0, 0, 2)
-        first_high = cast_w1(nc.scalar.copy, 0, 2, PACK)
-        low = cast_w1(nc.scalar.copy, 1, 0, 2)
-        high = cast_w1(nc.scalar.copy, 1, 2, PACK)
+        def cast_w1(copy, a, u):
+            copy(
+                w1_bf[u][:, :, a * MH : (a + 1) * MH, :].rearrange("p t m j -> p m j t"),
+                w1_raw[a][:].rearrange("p j (m t) -> p m j t", t=PACK)[:, :, :, 2 * u : 2 * u + 2],
+            )
+
+        cast_w1(nc.vector.tensor_copy, 0, 0)
+        cast_w1(nc.scalar.copy, 0, 1)
+        cast_w1(nc.scalar.copy, 1, 0)
+        cast_w1(nc.scalar.copy, 1, 1)
 
         w1_codes, w1_scales = [], []
         for t in range(PACK):
             codes = sb.tile([P, P], U32, name="w1_codes%d" % t, align_bytes=64)
             scales = sb.tile([P, P], U8, name="w1_scales%d" % t, align_bytes=64)
-            second = low[:, t] if t < 2 else high[:, t - 2]
-            first = first_low[:, t] if t < 2 else first_high[:, t - 2]
-            for a, part in enumerate((first, second)):
-                nc.vector.quantize_mx(codes[:, a * MH : (a + 1) * MH].bitcast(FP8X4), scales[:, a * MH : (a + 1) * MH],
-                                      part.rearrange("p m j -> p (m j)"))
+            for m0, m1 in ((0, MH), (MH, P)) if t < 2 else ((0, P),):
+                nc.vector.quantize_mx(codes[:, m0:m1].bitcast(FP8X4), scales[:, m0:m1],
+                                      w1_bf[t // 2][:, t % 2, m0:m1].rearrange("p m j -> p (m j)"))
             w1_codes.append(codes)
             w1_scales.append(scales)
 
         w2_codes = sb.tile([P, N], U32, name="w2_codes", align_bytes=64)
         w2_scales = sb.tile([P, N], U8, name="w2_scales", align_bytes=64)
         w2_first = sb.tile([P, P, PACK], BF16, name="w2_first", align_bytes=64)
-        w2_second = high[:, 0:2].rearrange("p t m j -> p (t m) j")
+        w2_second = w1_bf[1][:, 1]
         for m, (copy, w2_bf) in enumerate(((nc.scalar.copy, w2_first[:]), (nc.vector.tensor_copy, w2_second))):
             copy(
                 w2_bf.rearrange("p (c i) j -> p c j i", i=4),
@@ -97,30 +93,45 @@ def tile_picked_deepset_relu_p_kernel(tc, x_words, x_scales, w1, w2, offs, out):
         pairs = [sb.tile([P, PACK * 2 * CH], BF16, name="pairs%d" % g, align_bytes=64) for g in range(2)]
         hs = [sb.tile([P, S], F32, name="h%d" % t, align_bytes=64) for t in range(PACK)]
 
-        def product(t, n0, n1, bank, so_far=None):
-            acc = ps.tile([P, n1 - n0], F32, name="acc%d" % bank, tag="bank%d" % bank)
-            nc.tensor.matmul_mx(acc[:], lhsT=w1_codes[t][:].bitcast(FP8X4), lhsT_scale=w1_scales[t][:],
+        def multiply(t, acc, n0, n1):
+            nc.tensor.matmul_mx(acc, lhsT=w1_codes[t][:].bitcast(FP8X4), lhsT_scale=w1_scales[t][:],
                                 rhs=xg[:, n0:n1].bitcast(FP8X4), rhs_scale=xsg[:, n0:n1], start=True, stop=True)
-            total = sb.tile([P, 1], F32, name="total%d" % bank)
+
+        def rectify(t, acc, n0, n1, so_far=None):
+            total = sb.tile([P, 1], F32, name="total%d_%d" % (t, n0))
             if so_far is None:
-                nc.scalar.activation(hs[t][:, n0:n1], acc[:], ACT.Relu, accum_out=total[:])
+                nc.scalar.activation(hs[t][:, n0:n1], acc, ACT.Relu, accum_out=total[:])
             else:
-                nc.vector.tensor_scalar(hs[t][:, n0:n1], acc[:], 0.0, so_far[:], ALU.max, ALU.add, accum_out=total[:])
+                nc.vector.tensor_scalar(hs[t][:, n0:n1], acc, 0.0, so_far[:], ALU.max, ALU.add, accum_out=total[:])
             return total
+
+        def early(n0, bank):
+            accs = [ps.tile([P, SH], F32, name="acc%d" % (bank + t), tag="bank%d" % (bank + t)) for t in range(2)]
+            for n in range(0, SH, CH):
+                for t in range(2):
+                    multiply(t, accs[t][:, n : n + CH], n0 + n, n0 + n + CH)
+            return accs
+
+        def product(t):
+            acc = ps.tile([P, S], F32, name="acc%d" % t, tag="bank%d" % t)
+            multiply(t, acc[:], 0, S)
+            return rectify(t, acc[:], 0, S)
 
         def centre(t, total):
             for g in range(2):
                 nc.vector.tensor_scalar(pairs[g][:].rearrange("p (u n e) -> p u n e", u=2, e=2)[:, t // 2, :, t % 2],
                                         hs[t][:, g * 2 * CH : (g + 1) * 2 * CH], -float(S), total[:], ALU.mult, ALU.add)
 
-        parts = [product(t, 0, SH, 4 + t) for t in range(2)]
-        both_halves = [product(0, SH, S, 0, parts[0])]
-        rest = product(1, SH, S, 1)
+        accs = early(0, 4)
+        parts = [rectify(t, accs[t][:], 0, SH) for t in range(2)]
+        accs = early(SH, 0)
+        both_halves = [rectify(0, accs[0][:], SH, S, parts[0])]
+        rest = rectify(1, accs[1][:], SH, S)
         total = sb.tile([P, 1], F32, name="sum1")
         nc.vector.tensor_tensor(total[:], parts[1][:], rest[:], ALU.add)
         both_halves.append(total)
         for t in range(PACK):
-            centre(t, both_halves[t] if t < 2 else product(t, 0, S, t))
+            centre(t, both_halves[t] if t < 2 else product(t))
         spare = ps.tile([P, S], F32, name="spare", tag="bank6")
         nc.tensor.matmul_mx(spare[:], lhsT=w1_codes[3][:].bitcast(FP8X4), lhsT_scale=w1_scales[3][:],
                             rhs=xg[:].bitcast(FP8X4), rhs_scale=xsg[:], start=True, stop=True)
@@ -139,29 +150,26 @@ def tile_picked_deepset_relu_p_kernel(tc, x_words, x_scales, w1, w2, offs, out):
             else:
                 nc.vector.tensor_scalar(dst, src, -1.0 / S, None, ALU.mult)
 
+        sums = []
         for c in range(nch):
             z_codes = sb.tile([P, CH], U32, name="z_codes%d" % c, align_bytes=64)
             z_scales = sb.tile([P, CH], U8, name="z_scales%d" % c, align_bytes=64)
             nc.vector.quantize_mx(z_codes[:].bitcast(FP8X4), z_scales[:], zs[c][:])
-            if c in (0, nch - 1):
-                banks = [ps.tile([P, CH], F32, name="acc2_%d_%d" % (c, m), tag="bank%d" % (7 * m if c else 4 + m))[:] for m in range(2)]
-            else:
-                both = ps.tile([P, 2, CH], F32, name="acc2_%d" % c, tag="bank%d" % c)
-                banks = [both[:, m, :] for m in range(2)]
+            banks = [ps.tile([P, CH], F32, name="acc2_%d_%d" % (c, m), tag="bank%d" % ((2 * c + m + 4) % 8)) for m in range(2)]
             for m in range(2):
-                nc.tensor.matmul_mx(banks[m], lhsT=w2_codes[:, m * P : (m + 1) * P].bitcast(FP8X4),
+                nc.tensor.matmul_mx(banks[m][:], lhsT=w2_codes[:, m * P : (m + 1) * P].bitcast(FP8X4),
                                     lhsT_scale=w2_scales[:, m * P : (m + 1) * P],
                                     rhs=z_codes[:].bitcast(FP8X4), rhs_scale=z_scales[:], start=True, stop=True)
+            sums.append(banks)
+
+        for c, banks in enumerate(sums):
             if c == 0:
                 for m in range(2):
                     half = sb.tile([P, CH], F32, name="res0_%d" % m)
-                    leave("scalar", half[:], banks[m])
+                    leave("scalar", half[:], banks[m][:])
                     nc.sync.dma_start(out_rows[:, m, :CH], half[:])
                 continue
             res = sb.tile([P, 2, CH], F32, name="res%d" % c)
-            if c == nch - 1:
-                leave("scalar", res[:, 0, :], banks[0])
-                leave("vector", res[:, 1, :], banks[1])
-            else:
-                leave("scalar" if c < 2 else "vector", res[:], both[:])
+            leave("scalar", res[:, 0, :], banks[0][:])
+            leave("vector", res[:, 1, :], banks[1][:])
             nc.sync.dma_start(out_rows[:, :, c * CH : (c + 1) * CH], res[:])

@@ -70,7 +70,7 @@ def tile_picked_deepset_relu_p_kernel(tc, x_words, x_scales, w1, w2, offs, out):
         for t in range(PACK):
             codes = sb.tile([P, P], U32, name="w1_codes%d" % t, align_bytes=64)
             scales = sb.tile([P, P], U8, name="w1_scales%d" % t, align_bytes=64)
-            for m0, m1 in ((0, MH), (MH, P)) if t < 2 else ((0, P),):
+            for m0, m1 in ((0, MH), (MH, P)):
                 nc.vector.quantize_mx(codes[:, m0:m1].bitcast(FP8X4), scales[:, m0:m1],
                                       w1_bf[t // 2][:, t % 2, m0:m1].rearrange("p m j -> p (m j)"))
             w1_codes.append(codes)
@@ -150,26 +150,29 @@ def tile_picked_deepset_relu_p_kernel(tc, x_words, x_scales, w1, w2, offs, out):
             else:
                 nc.vector.tensor_scalar(dst, src, -1.0 / S, None, ALU.mult)
 
-        sums = []
         for c in range(nch):
             z_codes = sb.tile([P, CH], U32, name="z_codes%d" % c, align_bytes=64)
             z_scales = sb.tile([P, CH], U8, name="z_scales%d" % c, align_bytes=64)
             nc.vector.quantize_mx(z_codes[:].bitcast(FP8X4), z_scales[:], zs[c][:])
-            banks = [ps.tile([P, CH], F32, name="acc2_%d_%d" % (c, m), tag="bank%d" % ((2 * c + m + 4) % 8)) for m in range(2)]
+            if c in (0, nch - 1):
+                banks = [ps.tile([P, CH], F32, name="acc2_%d_%d" % (c, m), tag="bank%d" % (7 * m if c else 4 + m))[:] for m in range(2)]
+            else:
+                both = ps.tile([P, 2, CH], F32, name="acc2_%d" % c, tag="bank%d" % c)
+                banks = [both[:, m, :] for m in range(2)]
             for m in range(2):
-                nc.tensor.matmul_mx(banks[m][:], lhsT=w2_codes[:, m * P : (m + 1) * P].bitcast(FP8X4),
+                nc.tensor.matmul_mx(banks[m], lhsT=w2_codes[:, m * P : (m + 1) * P].bitcast(FP8X4),
                                     lhsT_scale=w2_scales[:, m * P : (m + 1) * P],
                                     rhs=z_codes[:].bitcast(FP8X4), rhs_scale=z_scales[:], start=True, stop=True)
-            sums.append(banks)
-
-        for c, banks in enumerate(sums):
             if c == 0:
                 for m in range(2):
                     half = sb.tile([P, CH], F32, name="res0_%d" % m)
-                    leave("scalar", half[:], banks[m][:])
+                    leave("scalar", half[:], banks[m])
                     nc.sync.dma_start(out_rows[:, m, :CH], half[:])
                 continue
             res = sb.tile([P, 2, CH], F32, name="res%d" % c)
-            leave("scalar", res[:, 0, :], banks[0][:])
-            leave("vector", res[:, 1, :], banks[1][:])
+            if c == nch - 1:
+                leave("scalar", res[:, 0, :], banks[0])
+                leave("vector", res[:, 1, :], banks[1])
+            else:
+                leave("scalar" if c < 2 else "vector", res[:], both[:])
             nc.sync.dma_start(out_rows[:, :, c * CH : (c + 1) * CH], res[:])

@@ -132,9 +132,6 @@ def tile_picked_deepset_relu_p_kernel(tc, x_words, x_scales, w1, w2, offs, out):
         both_halves.append(total)
         for t in range(PACK):
             centre(t, both_halves[t] if t < 2 else product(t))
-        spare = ps.tile([P, S], F32, name="spare", tag="bank6")
-        nc.tensor.matmul_mx(spare[:], lhsT=w1_codes[3][:].bitcast(FP8X4), lhsT_scale=w1_scales[3][:],
-                            rhs=xg[:].bitcast(FP8X4), rhs_scale=xsg[:], start=True, stop=True)
         out_rows = out.rearrange("(m p) n -> p m n", p=P)
         zs = []
         for c in range(nch):

@@ -67,9 +67,11 @@ def tile_picked_deepset_relu_p_kernel(tc, x_words, x_scales, w1, w2, offs, out):
         cast_w1(nc.scalar.copy, 1, 1)
 
         w1_codes, w1_scales = [], []
+        all_codes = sb.tile([P, H], U32, name="w1_codes", align_bytes=64)
+        all_scales = sb.tile([P, H], U8, name="w1_scales", align_bytes=64)
         for t in range(PACK):
-            codes = sb.tile([P, P], U32, name="w1_codes%d" % t, align_bytes=64)
-            scales = sb.tile([P, P], U8, name="w1_scales%d" % t, align_bytes=64)
+            codes = all_codes[:, t * P : (t + 1) * P]
+            scales = all_scales[:, t * P : (t + 1) * P]
             for m0, m1 in ((0, MH), (MH, P)):
                 nc.vector.quantize_mx(codes[:, m0:m1].bitcast(FP8X4), scales[:, m0:m1],
                                       w1_bf[t // 2][:, t % 2, m0:m1].rearrange("p m j -> p (m j)"))
@@ -94,7 +96,7 @@ def tile_picked_deepset_relu_p_kernel(tc, x_words, x_scales, w1, w2, offs, out):
         hs = [sb.tile([P, S], F32, name="h%d" % t, align_bytes=64) for t in range(PACK)]
 
         def multiply(t, acc, n0, n1):
-            nc.tensor.matmul_mx(acc, lhsT=w1_codes[t][:].bitcast(FP8X4), lhsT_scale=w1_scales[t][:],
+            nc.tensor.matmul_mx(acc, lhsT=w1_codes[t].bitcast(FP8X4), lhsT_scale=w1_scales[t],
                                 rhs=xg[:, n0:n1].bitcast(FP8X4), rhs_scale=xsg[:, n0:n1], start=True, stop=True)
 
         def rectify(t, acc, n0, n1, so_far=None):
@@ -132,6 +134,10 @@ def tile_picked_deepset_relu_p_kernel(tc, x_words, x_scales, w1, w2, offs, out):
         both_halves.append(total)
         for t in range(PACK):
             centre(t, both_halves[t] if t < 2 else product(t))
+        spare = ps.tile([32, S], F32, name="spare", tag="bank2")
+        for i in range(2):
+            nc.tensor.matmul_mx(spare[:], lhsT=all_codes[:, :32].bitcast(FP8X4), lhsT_scale=all_scales[:, :32],
+                                rhs=all_codes[:].bitcast(FP8X4), rhs_scale=all_scales[:], start=True, stop=True)
         out_rows = out.rearrange("(m p) n -> p m n", p=P)
         zs = []
         for c in range(nch):

@@ -29,15 +29,15 @@ def tile_picked_deepset_relu_p_kernel(tc, x_words, x_scales, w1, w2, offs, out):
         ps = ctx.enter_context(tc.psum_pool(name="ps", bufs=1))
 
         w1_rows = w1.rearrange("(p j) c -> p j c", j=PACK)
-        w1_raw = [sb.tile([P, PACK, HALF], F32, name="w1_raw%d" % a, align_bytes=64) for a in range(2)]
-        nc.sync.dma_start(w1_raw[0][:], w1_rows[:, :, :HALF])
+        w1_raw = sb.tile([P, PACK, H], F32, name="w1_raw", align_bytes=64)
+        nc.sync.dma_start(w1_raw[:, :2, :], w1_rows[:, :2, :])
         offsets = sb.tile([P, S // 16], U16, name="offsets")
         nc.sync.dma_start(offsets[:], offs)
         xs = sb.tile([P, T], U8, name="xs", align_bytes=64)
         nc.vector.memset(xs[:].bitcast(I32), 0)
         for q in range(4):
             nc.sync.dma_start(xs[32 * q : 32 * q + 4, :].bitcast(I32), x_scales[0, 4 * q : 4 * q + 4, :].bitcast(I32))
-        nc.sync.dma_start(w1_raw[1][:], w1_rows[:, :, HALF:])
+        nc.sync.dma_start(w1_raw[:, 2:, :], w1_rows[:, 2:, :])
         xw = sb.tile([P, T], I32, name="xw", align_bytes=64)
         nc.sync.dma_start(xw[:], x_words[0].rearrange("p c r -> p (c r)").bitcast(I32))
         w2_rows = w2.rearrange("(p j) c -> p j c", j=PACK)
@@ -53,35 +53,29 @@ def tile_picked_deepset_relu_p_kernel(tc, x_words, x_scales, w1, w2, offs, out):
 
         MH = HALF // PACK
 
-        w1_bf = [sb.tile([P, 2, P, PACK], BF16, name="w1_bf%d" % u, align_bytes=64) for u in range(2)]
+        w1_cols = w1_raw[:].rearrange("p j (m t) -> p m j t", t=PACK)
+        early_bf = [sb.tile([P, 2, MH, PACK], BF16, name="early_bf%d" % a, align_bytes=64) for a in range(2)]
+        late_bf = sb.tile([P, 2, P, PACK], BF16, name="late_bf", align_bytes=64)
+        nc.vector.tensor_copy(early_bf[0][:].rearrange("p t m j -> p m j t"), w1_cols[:, :MH, :, :2])
+        for j in range(0, PACK, 2):
+            nc.scalar.copy(early_bf[1][:].rearrange("p t m j -> p m j t")[:, :, j : j + 2, :], w1_cols[:, MH:, j : j + 2, :2])
+        nc.scalar.copy(late_bf[:].rearrange("p t m j -> p m j t"), w1_cols[:, :, :, 2:])
 
-        def cast_w1(copy, a, u):
-            copy(
-                w1_bf[u][:, :, a * MH : (a + 1) * MH, :].rearrange("p t m j -> p m j t"),
-                w1_raw[a][:].rearrange("p j (m t) -> p m j t", t=PACK)[:, :, :, 2 * u : 2 * u + 2],
-            )
-
-        cast_w1(nc.vector.tensor_copy, 0, 0)
-        cast_w1(nc.scalar.copy, 0, 1)
-        cast_w1(nc.scalar.copy, 1, 0)
-        cast_w1(nc.scalar.copy, 1, 1)
-
-        w1_codes, w1_scales = [], []
         all_codes = sb.tile([P, H], U32, name="w1_codes", align_bytes=64)
         all_scales = sb.tile([P, H], U8, name="w1_scales", align_bytes=64)
-        for t in range(PACK):
-            codes = all_codes[:, t * P : (t + 1) * P]
-            scales = all_scales[:, t * P : (t + 1) * P]
-            for m0, m1 in ((0, MH), (MH, P)):
-                nc.vector.quantize_mx(codes[:, m0:m1].bitcast(FP8X4), scales[:, m0:m1],
-                                      w1_bf[t // 2][:, t % 2, m0:m1].rearrange("p m j -> p (m j)"))
-            w1_codes.append(codes)
-            w1_scales.append(scales)
+        w1_codes = [all_codes[:, t * P : (t + 1) * P] for t in range(PACK)]
+        w1_scales = [all_scales[:, t * P : (t + 1) * P] for t in range(PACK)]
+        for a in (1, 0):
+            for t in range(2):
+                nc.vector.quantize_mx(w1_codes[t][:, a * MH : (a + 1) * MH].bitcast(FP8X4), w1_scales[t][:, a * MH : (a + 1) * MH],
+                                      early_bf[a][:, t].rearrange("p m j -> p (m j)"))
+        for t in range(2, PACK):
+            nc.vector.quantize_mx(w1_codes[t].bitcast(FP8X4), w1_scales[t], late_bf[:, t - 2].rearrange("p m j -> p (m j)"))
 
         w2_codes = sb.tile([P, N], U32, name="w2_codes", align_bytes=64)
         w2_scales = sb.tile([P, N], U8, name="w2_scales", align_bytes=64)
         w2_first = sb.tile([P, P, PACK], BF16, name="w2_first", align_bytes=64)
-        w2_second = w1_bf[1][:, 1]
+        w2_second = late_bf[:, 1]
         for m, (copy, w2_bf) in enumerate(((nc.scalar.copy, w2_first[:]), (nc.vector.tensor_copy, w2_second))):
             copy(
                 w2_bf.rearrange("p (c i) j -> p c j i", i=4),

from contextlib import ExitStack

import concourse.mybir as mybir

K, T, S, H, N = 512, 1024, 512, 512, 256
FLOPS = 2 * K * H * S + 2 * H * N * S

F32 = mybir.dt.float32
BF16 = mybir.dt.bfloat16
I32 = mybir.dt.int32
U32 = mybir.dt.uint32
U16 = mybir.dt.uint16
U8 = mybir.dt.uint8
FP8X4 = mybir.dt.float8_e4m3fn_x4
ALU = mybir.AluOpType
ACT = mybir.ActivationFunctionType

P = 128
PACK = 4
HALF = H // 2
CH = 128
SH = S // 2


def tile_picked_deepset_relu_p_kernel(tc, x_words, x_scales, w1, w2, offs, out):
    nc = tc.nc
    with ExitStack() as ctx:
        sb = ctx.enter_context(tc.tile_pool(name="sb", bufs=1))
        ps = ctx.enter_context(tc.psum_pool(name="ps", bufs=1))

        w1_rows = w1.rearrange("(p j) c -> p j c", j=PACK)
        w1_raw = sb.tile([P, PACK, H], F32, name="w1_raw", align_bytes=64)
        nc.sync.dma_start(w1_raw[:, :2, :], w1_rows[:, :2, :])
        offsets = sb.tile([P, S // 16], U16, name="offsets")
        nc.sync.dma_start(offsets[:], offs)
        xs = sb.tile([P, T], U8, name="xs", align_bytes=64)
        nc.vector.memset(xs[:].bitcast(I32), 0)
        for q in range(4):
            nc.sync.dma_start(xs[32 * q : 32 * q + 4, :].bitcast(I32), x_scales[0, 4 * q : 4 * q + 4, :].bitcast(I32))
        nc.sync.dma_start(w1_raw[:, 2:, :], w1_rows[:, 2:, :])
        xw = sb.tile([P, T], I32, name="xw", align_bytes=64)
        nc.sync.dma_start(xw[:], x_words[0].rearrange("p c r -> p (c r)").bitcast(I32))
        w2_rows = w2.rearrange("(p j) c -> p j c", j=PACK)
        w2_raw = [sb.tile([P, PACK, P], F32, name="w2_raw%d" % m, align_bytes=64) for m in range(2)]
        for m in range(2):
            nc.sync.dma_start(w2_raw[m][:], w2_rows[:, :, m * P : (m + 1) * P])

        xsg = sb.tile([P, S], U8, name="xsg", align_bytes=64)
        nc.vector.tensor_copy(xsg[:], xs[:].indirect(offsets[:]))
        xg = sb.tile([P, S], U32, name="xg", align_bytes=64)
        for n0 in range(0, S, CH):
            nc.vector.tensor_copy(xg[:, n0 : n0 + CH], xw[:].bitcast(U32).indirect(offsets[:, n0 // 16 : (n0 + CH) // 16]))

        MH = HALF // PACK

        w1_cols = w1_raw[:].rearrange("p j (m t) -> p m j t", t=PACK)
        early_bf = [sb.tile([P, 2, MH, PACK], BF16, name="early_bf%d" % a, align_bytes=64) for a in range(2)]
        late_bf = sb.tile([P, 2, P, PACK], BF16, name="late_bf", align_bytes=64)
        nc.vector.tensor_copy(early_bf[0][:].rearrange("p t m j -> p m j t"), w1_cols[:, :MH, :, :2])
        for j in range(0, PACK, 2):
            nc.scalar.copy(early_bf[1][:].rearrange("p t m j -> p m j t")[:, :, j : j + 2, :], w1_cols[:, MH:, j : j + 2, :2])
        nc.scalar.copy(late_bf[:].rearrange("p t m j -> p m j t"), w1_cols[:, :, :, 2:])

        all_codes = sb.tile([P, H], U32, name="w1_codes", align_bytes=64)
        all_scales = sb.tile([P, H], U8, name="w1_scales", align_bytes=64)
        w1_codes = [all_codes[:, t * P : (t + 1) * P] for t in range(PACK)]
        w1_scales = [all_scales[:, t * P : (t + 1) * P] for t in range(PACK)]
        for a in (1, 0):
            for t in range(2):
                nc.vector.quantize_mx(w1_codes[t][:, a * MH : (a + 1) * MH].bitcast(FP8X4), w1_scales[t][:, a * MH : (a + 1) * MH],
                                      early_bf[a][:, t].rearrange("p m j -> p (m j)"))
        for t in range(2, PACK):
            nc.vector.quantize_mx(w1_codes[t].bitcast(FP8X4), w1_scales[t], late_bf[:, t - 2].rearrange("p m j -> p (m j)"))

        w2_codes = sb.tile([P, N], U32, name="w2_codes", align_bytes=64)
        w2_scales = sb.tile([P, N], U8, name="w2_scales", align_bytes=64)
        w2_first = sb.tile([P, P, PACK], BF16, name="w2_first", align_bytes=64)
        w2_second = late_bf[:, 1]
        for m, (copy, w2_bf) in enumerate(((nc.scalar.copy, w2_first[:]), (nc.vector.tensor_copy, w2_second))):
            copy(
                w2_bf.rearrange("p (c i) j -> p c j i", i=4),
                w2_raw[m][:].rearrange("p j (c i) -> p c j i", i=4),
            )
        for m, w2_bf in ((0, w2_first[:]), (1, w2_second)):
            nc.vector.quantize_mx(w2_codes[:, m * P : (m + 1) * P].bitcast(FP8X4), w2_scales[:, m * P : (m + 1) * P],
                                  w2_bf.rearrange("p c j -> p (c j)"))

        nch = S // CH
        pairs = [sb.tile([P, PACK * 2 * CH], BF16, name="pairs%d" % g, align_bytes=64) for g in range(2)]
        hs = [sb.tile([P, S], F32, name="h%d" % t, align_bytes=64) for t in range(PACK)]

        def multiply(t, acc, n0, n1):
            nc.tensor.matmul_mx(acc, lhsT=w1_codes[t].bitcast(FP8X4), lhsT_scale=w1_scales[t],
                                rhs=xg[:, n0:n1].bitcast(FP8X4), rhs_scale=xsg[:, n0:n1], start=True, stop=True)

        def rectify(t, acc, n0, n1, so_far=None):
            total = sb.tile([P, 1], F32, name="total%d_%d" % (t, n0))
            if so_far is None:
                nc.scalar.activation(hs[t][:, n0:n1], acc, ACT.Relu, accum_out=total[:])
            else:
                nc.vector.tensor_scalar(hs[t][:, n0:n1], acc, 0.0, so_far[:], ALU.max, ALU.add, accum_out=total[:])
            return total

        def early(n0, bank):
            accs = [ps.tile([P, SH], F32, name="acc%d" % (bank + t), tag="bank%d" % (bank + t)) for t in range(2)]
            for n in range(0, SH, CH):
                for t in range(2):
                    multiply(t, accs[t][:, n : n + CH], n0 + n, n0 + n + CH)
            return accs

        def product(t):
            acc = ps.tile([P, S], F32, name="acc%d" % t, tag="bank%d" % t)
            multiply(t, acc[:], 0, S)
            return rectify(t, acc[:], 0, S)

        def centre(t, total):
            for g in range(2):
                nc.vector.tensor_scalar(pairs[g][:].rearrange("p (u n e) -> p u n e", u=2, e=2)[:, t // 2, :, t % 2],
                                        hs[t][:, g * 2 * CH : (g + 1) * 2 * CH], -float(S), total[:], ALU.mult, ALU.add)

        accs = early(0, 4)
        parts = [rectify(t, accs[t][:], 0, SH) for t in range(2)]
        accs = early(SH, 0)
        both_halves = [rectify(0, accs[0][:], SH, S, parts[0])]
        rest = rectify(1, accs[1][:], SH, S)
        total = sb.tile([P, 1], F32, name="sum1")
        nc.vector.tensor_tensor(total[:], parts[1][:], rest[:], ALU.add)
        both_halves.append(total)
        for t in range(PACK):
            centre(t, both_halves[t] if t < 2 else product(t))
        spare = ps.tile([32, S], F32, name="spare", tag="bank2")
        for i in range(2):
            nc.tensor.matmul_mx(spare[:], lhsT=all_codes[:, :32].bitcast(FP8X4), lhsT_scale=all_scales[:, :32],
                                rhs=all_codes[:].bitcast(FP8X4), rhs_scale=all_scales[:], start=True, stop=True)
        out_rows = out.rearrange("(m p) n -> p m n", p=P)
        zs = []
        for c in range(nch):
            z = sb.tile([P, CH * PACK], BF16, name="z%d" % c, align_bytes=64)
            copy = nc.vector.tensor_copy if c % 2 == 0 else nc.scalar.copy
            copy(z[:].bitcast(F32).rearrange("p (n u) -> p n u", u=2),
                 pairs[c // 2][:].bitcast(F32).rearrange("p (u n) -> p n u", u=2)[:, c % 2 * CH : (c % 2 + 1) * CH, :])
            zs.append(z)

        def leave(engine, dst, src):
            if engine == "scalar":
                nc.scalar.activation(dst, src, ACT.Copy, scale=-1.0 / S)
            else:
                nc.vector.tensor_scalar(dst, src, -1.0 / S, None, ALU.mult)

        for c in range(nch):
            z_codes = sb.tile([P, CH], U32, name="z_codes%d" % c, align_bytes=64)
            z_scales = sb.tile([P, CH], U8, name="z_scales%d" % c, align_bytes=64)
            nc.vector.quantize_mx(z_codes[:].bitcast(FP8X4), z_scales[:], zs[c][:])
            if c in (0, nch - 1):
                banks = [ps.tile([P, CH], F32, name="acc2_%d_%d" % (c, m), tag="bank%d" % (7 * m if c else 4 + m))[:] for m in range(2)]
            else:
                both = ps.tile([P, 2, CH], F32, name="acc2_%d" % c, tag="bank%d" % c)
                banks = [both[:, m, :] for m in range(2)]
            for m in range(2):
                nc.tensor.matmul_mx(banks[m], lhsT=w2_codes[:, m * P : (m + 1) * P].bitcast(FP8X4),
                                    lhsT_scale=w2_scales[:, m * P : (m + 1) * P],
                                    rhs=z_codes[:].bitcast(FP8X4), rhs_scale=z_scales[:], start=True, stop=True)
            if c == 0:
                for m in range(2):
                    half = sb.tile([P, CH], F32, name="res0_%d" % m)
                    leave("scalar", half[:], banks[m])
                    nc.sync.dma_start(out_rows[:, m, :CH], half[:])
                continue
            res = sb.tile([P, 2, CH], F32, name="res%d" % c)
            if c == nch - 1:
                leave("scalar", res[:, 0, :], banks[0])
                leave("vector", res[:, 1, :], banks[1])
            else:
                leave("scalar" if c < 2 else "vector", res[:], both[:])
            nc.sync.dma_start(out_rows[:, :, c * CH : (c + 1) * CH], res[:])
